import numpy as np
import ml_dtypes


def mxq(x, axis, fmt="e4m3"):
    dtype, down = {"e4m3": (ml_dtypes.float8_e4m3fn, 7), "e5m2": (ml_dtypes.float8_e5m2, 14)}[fmt]
    v = np.moveaxis(np.asarray(x, np.float32).astype(ml_dtypes.bfloat16).astype(np.float64), axis, -1)
    blocks = v.reshape(v.shape[:-1] + (-1, 32))
    amax = np.abs(blocks).max(-1, keepdims=True)
    byte = np.maximum(np.where(amax > 0, np.frexp(amax)[1] - 1 + 127, 0) - down, 1)
    scale = np.exp2(byte - 127.0)
    codes = (blocks / scale).astype(np.float32).astype(dtype).astype(np.float64)
    return np.moveaxis((codes * scale).reshape(v.shape), -1, axis)


WIDE = False


def mx_kscale(k):
    if not WIDE:
        return np.ones(k)
    levels = np.array([10, -10, 5, -5, 0])
    if k % 512:
        return np.exp2(np.random.permutation(np.resize(levels, k // 32))).repeat(32)
    a = np.empty((k // 512, 16))
    for p in range(k // 512):
        a[p, :8] = np.random.permutation(np.resize(levels, 8))
        for g in range(8):
            far = levels[np.abs(levels - a[p, g]) >= 10]
            a[p, g + 8] = far[np.random.randint(len(far))]
    return np.exp2(a.ravel()).repeat(32)


def f64(x):
    return np.asarray(x).astype(np.float64)


def striped(idx):
    return np.tile(idx.reshape(-1, 16).T, (8, 1)).astype(np.uint16)


def unstriped(offs):
    return offs[:16].T.reshape(-1).astype(np.int64)


E2M1 = np.array([0.0, 0.5, 1.0, 1.5, 2.0, 3.0, 4.0, 6.0, -0.0, -0.5, -1.0, -1.5, -2.0, -3.0, -4.0, -6.0])


def pack_weight(w, fmt):
    k, n = w.shape
    w = f64(np.asarray(w, np.float32).astype(ml_dtypes.bfloat16)).reshape(k // 32, 32, n)
    amax = np.abs(w).max(1)
    if fmt == "e4m3":
        byte = np.frexp(amax)[1] - 1 + 127 - 7
    else:
        mant, ex = np.frexp(amax / 6.0)
        byte = np.where(mant > 0.5, ex, ex - 1) + 127
    byte = np.clip(np.where(amax > 0, byte, 1), 1, 254)
    scaled = (w * np.exp2(127.0 - byte)[:, None, :]).reshape(k, n).astype(np.float32)
    by_word = np.ascontiguousarray(scaled.reshape(k // 512, 128, 4, n).transpose(0, 1, 3, 2))
    if fmt == "e4m3":
        words = by_word.astype(ml_dtypes.float8_e4m3fn).view(np.uint8)
    else:
        c = by_word.astype(ml_dtypes.float4_e2m1fn).view(np.uint8) & 0xF
        words = (c[..., 0::2] | (c[..., 1::2] << 4)).reshape(k // 512, 128, 2 * n)
    return np.ascontiguousarray(words), np.ascontiguousarray(byte.astype(np.uint8).reshape(k // 512, 16, n))


def unpack_weight(words, scales, fmt):
    g, _, n = scales.shape
    words = np.ascontiguousarray(words).reshape(g, 128, n, -1)
    if fmt == "e4m3":
        vals = words.view(ml_dtypes.float8_e4m3fn).astype(np.float64)
    else:
        nib = np.empty((g, 128, n, 4), np.uint8)
        nib[..., 0::2] = words & 0xF
        nib[..., 1::2] = words >> 4
        vals = E2M1[nib]
    vals = vals * np.repeat(np.exp2(scales.astype(np.float64) - 127.0), 8, axis=1)[..., None]
    return vals.transpose(0, 1, 3, 2).reshape(g * 512, n)


def gelu(v):
    return 0.5 * v * (1.0 + np.tanh(np.sqrt(2.0 / np.pi) * (v + 0.044715 * v**3)))


K, T, E, C, H, N = 512, 2048, 8, 256, 512, 128
TOP = 3
PAD = 64


def by_expert(wq, xq):
    return np.concatenate([wq[e].T @ xq[:, e * C:(e + 1) * C] for e in range(E)], axis=1)


def setup_inputs():
    n = np.random.standard_normal
    s = mx_kscale(K)[:, None]
    u = mx_kscale(H)
    slot_token = np.empty(E * C, np.int64); pos = np.tile(E * C + np.arange(T) % PAD, (TOP, 1)); taken = np.zeros(T, np.int64)
    liked = np.random.randn(T)
    for e in np.random.permutation(E):
        free = np.flatnonzero(taken < TOP); pick = np.random.permutation(free[np.argsort(-(liked[free] + np.random.gumbel(size=free.size)))[:C]]); slot_token[e * C:(e + 1) * C] = pick
        pos[taken[pick], pick] = e * C + np.arange(C); taken[pick] += 1
    g = np.random.uniform(0.2, 0.8, (TOP, T))
    x = pack_weight(n((K, T)) * s, "e4m3")
    return {
        "x_words": x[0],
        "x_scales": x[1],
        "w1": (n((E, K, H)) / np.sqrt(K) / s[None]).astype(np.float32),
        "w3": (n((E, K, H)) / np.sqrt(K) / s[None] * u[None, None, :]).astype(np.float32),
        "w2": (n((E, H, N)) / np.sqrt(H) / u[None, :, None]).astype(np.float32),
        "gate": np.stack([np.tile(r, (N, 1)) for r in g]).astype(np.float32),
        "offs": striped(slot_token),
        "pos1": striped(pos[0]),
        "pos2": striped(pos[1]),
        "pos3": striped(pos[2]),
    }


def reference(x_words, x_scales, w1, w3, w2, gate, offs, pos1, pos2, pos3):
    idx = unstriped(offs)
    xq = unpack_weight(x_words, x_scales, "e4m3")[:, idx]
    h = gelu(by_expert(mxq(f64(w1), 1, "e4m3"), xq))
    h = h * by_expert(mxq(f64(w3), 1, "e4m3"), xq)
    y = by_expert(mxq(f64(w2), 1, "e4m3"), mxq(h, 0, "e4m3"))
    y = np.concatenate([y, np.zeros((N, PAD))], axis=1)
    return sum(f64(gate[r]) * y[:, unstriped(p)] for r, p in enumerate((pos1, pos2, pos3)))

@@ -1,0 +1,204 @@
+from contextlib import ExitStack
+
+import concourse.mybir as mybir
+from concourse.masks import make_identity
+
+K, T, E, C, H, N = 512, 2048, 8, 256, 512, 128
+TOP = 3
+PAD = 64
+S = E * C
+P = 128
+PACK = 4
+
+FLOPS = 2 * S * (2 * K * H + H * N)
+BYTES = 4 * E * (2 * K * H + H * N) + K * T + 16 * T + 4 * TOP * T + 4 * 2 * P * (T // 16) + 4 * N * T
+
+F32 = mybir.dt.float32
+BF16 = mybir.dt.bfloat16
+I32 = mybir.dt.int32
+U32 = mybir.dt.uint32
+U16 = mybir.dt.uint16
+U8 = mybir.dt.uint8
+FP8X4 = mybir.dt.float8_e4m3fn_x4
+MULT = mybir.AluOpType.mult
+ADD = mybir.AluOpType.add
+GELU = mybir.ActivationFunctionType.Gelu_apprx_tanh
+
+GATHER = 1024
+CHUNKS = (512, 512, 512, 256, 256)
+AHEAD = 2
+
+
+def tile_moe_ecr_glu_gelu_kernel(tc, x_words, x_scales, w1, w3, w2, gate, offs, pos1, pos2, pos3, out):
+    nc = tc.nc
+    with ExitStack() as ctx:
+        keep = ctx.enter_context(tc.tile_pool(name="keep", bufs=1))
+        ring = ctx.enter_context(tc.tile_pool(name="ring", bufs=12))
+        work = ctx.enter_context(tc.tile_pool(name="work", bufs=3))
+        psum = ctx.enter_context(tc.psum_pool(name="psum", bufs=3))
+        psum_y = ctx.enter_context(tc.psum_pool(name="psum_y", bufs=2))
+
+        slot_list = keep.tile([P, S // 16], U16, name="slot_list")
+        nc.sync.dma_start(slot_list[:], offs)
+
+        tok_scales = keep.tile([P, T], U8, name="tok_scales", align_bytes=64)
+        nc.vector.memset(tok_scales[:].bitcast(I32), 0)
+        landed = keep.tile([P, T], U8, name="landed", align_bytes=64)
+        for q in range(4):
+            rows = slice(32 * q, 32 * q + 4)
+            nc.sync.dma_start(landed[rows, :].bitcast(I32), x_scales[0, 4 * q : 4 * q + 4, :].bitcast(I32))
+            nc.vector.tensor_copy(tok_scales[rows, :].bitcast(I32), landed[rows, :].bitcast(I32))
+
+        y = keep.tile([P, S + PAD], F32, name="y")
+        zeros = keep.tile([P, PAD], F32, name="zeros")
+        nc.vector.memset(zeros[:], 0.0)
+        nc.scalar.activation(y[:, S:], zeros[:], GELU)
+
+        raw = {}
+
+        def load_first(name, w, e):
+            raw[name, e] = ring.tile([P, PACK, H], F32, name="raw", tag="raw")
+            nc.sync.dma_start(raw[name, e][:], w[e].rearrange("(p j) c -> p j c", j=PACK))
+
+        def load_second(e):
+            raw["w2", e] = ring.tile([P, PACK * N], F32, name="raw", tag="raw")
+            nc.sync.dma_start(raw["w2", e][:], w2[e].rearrange("(p j) n -> p (j n)", j=PACK))
+
+        def load_expert(e):
+            load_first("w1", w1, e)
+            load_first("w3", w3, e)
+            load_second(e)
+
+        load_first("w1", w1, 0)
+        tok_words = keep.tile([P, T], I32, name="tok_words", align_bytes=64)
+        nc.sync.dma_start(tok_words[:], x_words[0].rearrange("p t r -> p (t r)").bitcast(I32))
+        load_first("w3", w3, 0)
+        load_second(0)
+        for e in range(1, AHEAD):
+            load_expert(e)
+
+        slot_words, slot_scales = [], []
+        for g in range(S // GATHER):
+            piece = slot_list[:, g * GATHER // 16 : (g + 1) * GATHER // 16]
+            slot_scales.append(keep.tile([P, GATHER], U8, name="slot_scales%d" % g, align_bytes=64))
+            nc.vector.tensor_copy(slot_scales[g][:], tok_scales[:].indirect(piece))
+        for g in range(S // GATHER):
+            piece = slot_list[:, g * GATHER // 16 : (g + 1) * GATHER // 16]
+            slot_words.append(keep.tile([P, GATHER], U32, name="slot_words%d" % g, align_bytes=64))
+            nc.vector.tensor_copy(slot_words[g][:], tok_words[:].bitcast(U32).indirect(piece))
+
+        def quantise(values, width, tag):
+            codes = work.tile([P, width], U32, name="codes", tag=tag + "_codes", align_bytes=64)
+            scales = work.tile([P, width], U8, name="scales", tag=tag + "_scales", align_bytes=64)
+            nc.vector.quantize_mx(out=codes[:].bitcast(FP8X4), scales=scales[:], in_=values[:])
+            return codes, scales
+
+        def first_matrix(name, e, copy):
+            rounded = work.tile([P, PACK * H], BF16, name="rounded", tag=name + "_bf16", align_bytes=64)
+            copy(
+                rounded[:].rearrange("p (t m j) -> p m j t", t=PACK, j=PACK),
+                raw[name, e][:].rearrange("p j (m t) -> p m j t", t=PACK),
+            )
+            return quantise(rounded, H, name)
+
+        def first_product(weights, slot0, tag):
+            codes, scales = weights
+            bank = psum.tile([P, PACK, P], F32, name="bank", tag=tag)
+            g, c0 = divmod(slot0, GATHER)
+            for t in range(PACK):
+                nc.tensor.matmul_mx(
+                    out=bank[:, t, :],
+                    lhsT=codes[:, t * P : (t + 1) * P].bitcast(FP8X4),
+                    lhsT_scale=scales[:, t * P : (t + 1) * P],
+                    rhs=slot_words[g][:, c0 : c0 + P].bitcast(FP8X4),
+                    rhs_scale=slot_scales[g][:, c0 : c0 + P],
+                    start=True,
+                    stop=True,
+                )
+            return bank
+
+        def hidden(e):
+            q1 = first_matrix("w1", e, nc.scalar.copy if e in (0, E - 1) else nc.vector.tensor_copy)
+            q3 = first_matrix("w3", e, nc.vector.tensor_copy if e == E - 1 else nc.scalar.copy)
+            h = work.tile([P, C * PACK], BF16, name="h", align_bytes=64)
+            for half in range(C // P):
+                a1 = first_product(q1, e * C + half * P, "a1")
+                a3 = first_product(q3, e * C + half * P, "a3")
+                act = work.tile([P, P, PACK], F32, name="act")
+                nc.scalar.activation(act[:], a1[:].rearrange("p t s -> p s t"), GELU)
+                nc.vector.tensor_tensor(
+                    h[:, half * P * PACK : (half + 1) * P * PACK].rearrange("p (s t) -> p s t", t=PACK),
+                    a3[:].rearrange("p t s -> p s t"),
+                    act[:],
+                    MULT,
+                )
+            return quantise(h, C, "h")
+
+        def second_product(e, hq):
+            rounded = work.tile([P, PACK * N], BF16, name="rounded2", align_bytes=64)
+            nc.scalar.copy(
+                rounded[:].rearrange("p (c i j) -> p c j i", i=4, j=PACK),
+                raw["w2", e][:].rearrange("p (j c i) -> p c j i", i=4, j=PACK),
+            )
+            codes, scales = quantise(rounded, N, "w2")
+            bank = psum_y.tile([P, C], F32, name="bank_y")
+            nc.tensor.matmul_mx(
+                out=bank[:],
+                lhsT=codes[:].bitcast(FP8X4),
+                lhsT_scale=scales[:],
+                rhs=hq[0][:].bitcast(FP8X4),
+                rhs_scale=hq[1][:],
+                start=True,
+                stop=True,
+            )
+            nc.scalar.copy(y[:, e * C : (e + 1) * C], bank[:])
+
+        hq = {}
+        for e in range(E):
+            if e + AHEAD < E:
+                load_expert(e + AHEAD)
+            hq[e] = hidden(e)
+            second_product(e, hq[e])
+
+        lists = []
+        for r, pos in enumerate((pos1, pos2, pos3)):
+            lists.append(keep.tile([P, T // 16], U16, name="pos%d" % r))
+            nc.sync.dma_start(lists[r][:], pos)
+        ident = keep.tile([P, P], F32, name="ident")
+        make_identity(nc, ident[:])
+
+        t0 = 0
+        for n, width in enumerate(CHUNKS):
+            gates = ring.tile([P, TOP, width], F32, name="raw", tag="raw")
+            nc.sync.dma_start(gates[:], gate[:, :, t0 : t0 + width].rearrange("r p t -> p r t"))
+            terms = []
+            for r in range(TOP):
+                terms.append(work.tile([P, width], F32, name="term", tag="term%d" % r))
+                nc.vector.tensor_tensor(
+                    terms[r][:], y[:].indirect(lists[r][:, t0 // 16 : (t0 + width) // 16]), gates[:, r, :], MULT
+                )
+            result = work.tile([P, width], F32, name="result")
+            if n + 1 < len(CHUNKS):
+                turned = psum.tile([P, width], F32, name="turned", tag="a1")
+                for b in range(width // P):
+                    for r in range(TOP):
+                        nc.tensor.matmul(
+                            turned[:, b * P : (b + 1) * P],
+                            terms[r][:, b * P : (b + 1) * P],
+                            ident[:],
+                            start=(r == 0),
+                            stop=(r == TOP - 1),
+                            is_transpose=True,
+                        )
+                summed = work.tile([P, width], F32, name="summed")
+                nc.scalar.copy(summed[:], turned[:])
+                back = psum.tile([P, width], F32, name="back", tag="a3")
+                for b in range(width // P):
+                    nc.tensor.transpose(back[:, b * P : (b + 1) * P], summed[:, b * P : (b + 1) * P], ident[:])
+                nc.scalar.copy(result[:], back[:])
+            else:
+                pair = work.tile([P, width], F32, name="pair")
+                nc.vector.tensor_tensor(pair[:], terms[0][:], terms[1][:], ADD)
+                nc.vector.tensor_tensor(result[:], pair[:], terms[2][:], ADD)
+            nc.sync.dma_start(out[:, t0 : t0 + width], result[:])
+            t0 = t0 + width

@@ -27,6 +27,7 @@ GELU = mybir.ActivationFunctionType.Gelu_apprx_tanh
 GATHER = 1024
 CHUNKS = (512, 512, 512, 256, 256)
 AHEAD = 2
+LAG = 3
 
 
 def tile_moe_ecr_glu_gelu_kernel(tc, x_words, x_scales, w1, w3, w2, gate, offs, pos1, pos2, pos3, out):
@@ -57,8 +58,13 @@ def tile_moe_ecr_glu_gelu_kernel(tc, x_words, x_scales, w1, w3, w2, gate, offs, 
         raw = {}
 
         def load_first(name, w, e):
-            raw[name, e] = ring.tile([P, PACK, H], F32, name="raw", tag="raw")
-            nc.sync.dma_start(raw[name, e][:], w[e].rearrange("(p j) c -> p j c", j=PACK))
+            rows = w[e].rearrange("(p j) c -> p j c", j=PACK)
+            parts = 2 if (name, e) == ("w3", E - 1) else 1
+            raw[name, e] = []
+            for part in range(parts):
+                tile = ring.tile([P, PACK, H // parts], F32, name="raw", tag="raw")
+                nc.sync.dma_start(tile[:], rows[:, :, part * H // parts : (part + 1) * H // parts])
+                raw[name, e].append(tile)
 
         def load_second(e):
             raw["w2", e] = ring.tile([P, PACK * N], F32, name="raw", tag="raw")
@@ -67,13 +73,16 @@ def tile_moe_ecr_glu_gelu_kernel(tc, x_words, x_scales, w1, w3, w2, gate, offs, 
         def load_expert(e):
             load_first("w1", w1, e)
             load_first("w3", w3, e)
-            load_second(e)
+            if e >= LAG:
+                load_second(e - LAG)
+            if e == E - 1:
+                for late in range(E - LAG, E):
+                    load_second(late)
 
         load_first("w1", w1, 0)
+        load_first("w3", w3, 0)
         tok_words = keep.tile([P, T], I32, name="tok_words", align_bytes=64)
         nc.sync.dma_start(tok_words[:], x_words[0].rearrange("p t r -> p (t r)").bitcast(I32))
-        load_first("w3", w3, 0)
-        load_second(0)
         for e in range(1, AHEAD):
             load_expert(e)
 
@@ -87,18 +96,21 @@ def tile_moe_ecr_glu_gelu_kernel(tc, x_words, x_scales, w1, w3, w2, gate, offs, 
             slot_words.append(keep.tile([P, GATHER], U32, name="slot_words%d" % g, align_bytes=64))
             nc.vector.tensor_copy(slot_words[g][:], tok_words[:].bitcast(U32).indirect(piece))
 
-        def quantise(values, width, tag):
-            codes = work.tile([P, width], U32, name="codes", tag=tag + "_codes", align_bytes=64)
-            scales = work.tile([P, width], U8, name="scales", tag=tag + "_scales", align_bytes=64)
+        def quantise(values, width, tag, depth=3):
+            codes = work.tile([P, width], U32, name="codes", tag=tag + "_codes", align_bytes=64, bufs=depth)
+            scales = work.tile([P, width], U8, name="scales", tag=tag + "_scales", align_bytes=64, bufs=depth)
             nc.vector.quantize_mx(out=codes[:].bitcast(FP8X4), scales=scales[:], in_=values[:])
             return codes, scales
 
-        def first_matrix(name, e, copy):
+        def first_matrix(name, e, copies):
             rounded = work.tile([P, PACK * H], BF16, name="rounded", tag=name + "_bf16", align_bytes=64)
-            copy(
-                rounded[:].rearrange("p (t m j) -> p m j t", t=PACK, j=PACK),
-                raw[name, e][:].rearrange("p j (m t) -> p m j t", t=PACK),
-            )
+            turned = rounded[:].rearrange("p (t m j) -> p m j t", t=PACK, j=PACK)
+            share = P // len(copies)
+            for part, copy in enumerate(copies):
+                copy(
+                    turned[:, part * share : (part + 1) * share],
+                    raw[name, e][part][:].rearrange("p j (m t) -> p m j t", t=PACK),
+                )
             return quantise(rounded, H, name)
 
         def first_product(weights, slot0, tag):
@@ -117,9 +129,12 @@ def tile_moe_ecr_glu_gelu_kernel(tc, x_words, x_scales, w1, w3, w2, gate, offs, 
                 )
             return bank
 
-        def hidden(e):
-            q1 = first_matrix("w1", e, nc.scalar.copy if e in (0, E - 1) else nc.vector.tensor_copy)
-            q3 = first_matrix("w3", e, nc.vector.tensor_copy if e == E - 1 else nc.scalar.copy)
+        def first_weights(e):
+            q1 = first_matrix("w1", e, [nc.scalar.copy if e == 0 else nc.vector.tensor_copy])
+            q3 = first_matrix("w3", e, [nc.scalar.copy, nc.vector.tensor_copy] if e == E - 1 else [nc.scalar.copy])
+            return q1, q3
+
+        def hidden(e, q1, q3):
             h = work.tile([P, C * PACK], BF16, name="h", align_bytes=64)
             for half in range(C // P):
                 a1 = first_product(q1, e * C + half * P, "a1")
@@ -132,7 +147,7 @@ def tile_moe_ecr_glu_gelu_kernel(tc, x_words, x_scales, w1, w3, w2, gate, offs, 
                     act[:],
                     MULT,
                 )
-            return quantise(h, C, "h")
+            return quantise(h, C, "h", LAG + 2)
 
         def second_product(e, hq):
             rounded = work.tile([P, PACK * N], BF16, name="rounded2", align_bytes=64)
@@ -154,10 +169,16 @@ def tile_moe_ecr_glu_gelu_kernel(tc, x_words, x_scales, w1, w3, w2, gate, offs, 
             nc.scalar.copy(y[:, e * C : (e + 1) * C], bank[:])
 
         hq = {}
+        wq = {0: first_weights(0)}
         for e in range(E):
             if e + AHEAD < E:
                 load_expert(e + AHEAD)
-            hq[e] = hidden(e)
+            if e + 1 < E:
+                wq[e + 1] = first_weights(e + 1)
+            hq[e] = hidden(e, *wq[e])
+            if e >= LAG:
+                second_product(e - LAG, hq[e - LAG])
+        for e in range(E - LAG, E):
             second_product(e, hq[e])
 
         lists = []

from contextlib import ExitStack

import concourse.mybir as mybir
from concourse.masks import make_identity

K, T, E, C, H, N = 512, 2048, 8, 256, 512, 128
TOP = 3
PAD = 64
S = E * C
P = 128
PACK = 4

FLOPS = 2 * S * (2 * K * H + H * N)
BYTES = 4 * E * (2 * K * H + H * N) + K * T + 16 * T + 4 * TOP * T + 4 * 2 * P * (T // 16) + 4 * N * T

F32 = mybir.dt.float32
BF16 = mybir.dt.bfloat16
I32 = mybir.dt.int32
U32 = mybir.dt.uint32
U16 = mybir.dt.uint16
U8 = mybir.dt.uint8
FP8X4 = mybir.dt.float8_e4m3fn_x4
MULT = mybir.AluOpType.mult
ADD = mybir.AluOpType.add
GELU = mybir.ActivationFunctionType.Gelu_apprx_tanh

GATHER = 1024
CHUNKS = (512, 512, 512, 256, 256)
AHEAD = 2
LAG = 3


def tile_moe_ecr_glu_gelu_kernel(tc, x_words, x_scales, w1, w3, w2, gate, offs, pos1, pos2, pos3, out):
    nc = tc.nc
    with ExitStack() as ctx:
        keep = ctx.enter_context(tc.tile_pool(name="keep", bufs=1))
        ring = ctx.enter_context(tc.tile_pool(name="ring", bufs=12))
        work = ctx.enter_context(tc.tile_pool(name="work", bufs=3))
        psum = ctx.enter_context(tc.psum_pool(name="psum", bufs=3))
        psum_y = ctx.enter_context(tc.psum_pool(name="psum_y", bufs=2))

        slot_list = keep.tile([P, S // 16], U16, name="slot_list")
        nc.sync.dma_start(slot_list[:], offs)

        tok_scales = keep.tile([P, T], U8, name="tok_scales", align_bytes=64)
        nc.vector.memset(tok_scales[:].bitcast(I32), 0)
        landed = keep.tile([P, T], U8, name="landed", align_bytes=64)
        for q in range(4):
            rows = slice(32 * q, 32 * q + 4)
            nc.sync.dma_start(landed[rows, :].bitcast(I32), x_scales[0, 4 * q : 4 * q + 4, :].bitcast(I32))
            nc.vector.tensor_copy(tok_scales[rows, :].bitcast(I32), landed[rows, :].bitcast(I32))

        y = keep.tile([P, S + PAD], F32, name="y")
        zeros = keep.tile([P, PAD], F32, name="zeros")
        nc.vector.memset(zeros[:], 0.0)
        nc.scalar.activation(y[:, S:], zeros[:], GELU)

        raw = {}

        def load_first(name, w, e):
            rows = w[e].rearrange("(p j) c -> p j c", j=PACK)
            parts = 2 if (name, e) == ("w3", E - 1) else 1
            raw[name, e] = []
            for part in range(parts):
                tile = ring.tile([P, PACK, H // parts], F32, name="raw", tag="raw")
                nc.sync.dma_start(tile[:], rows[:, :, part * H // parts : (part + 1) * H // parts])
                raw[name, e].append(tile)

        def load_second(e):
            raw["w2", e] = ring.tile([P, PACK * N], F32, name="raw", tag="raw")
            nc.sync.dma_start(raw["w2", e][:], w2[e].rearrange("(p j) n -> p (j n)", j=PACK))

        def load_expert(e):
            load_first("w1", w1, e)
            load_first("w3", w3, e)
            if e >= LAG:
                load_second(e - LAG)
            if e == E - 1:
                for late in range(E - LAG, E):
                    load_second(late)

        load_first("w1", w1, 0)
        load_first("w3", w3, 0)
        tok_words = keep.tile([P, T], I32, name="tok_words", align_bytes=64)
        nc.sync.dma_start(tok_words[:], x_words[0].rearrange("p t r -> p (t r)").bitcast(I32))
        for e in range(1, AHEAD):
            load_expert(e)

        slot_words, slot_scales = [], []
        for g in range(S // GATHER):
            piece = slot_list[:, g * GATHER // 16 : (g + 1) * GATHER // 16]
            slot_scales.append(keep.tile([P, GATHER], U8, name="slot_scales%d" % g, align_bytes=64))
            nc.vector.tensor_copy(slot_scales[g][:], tok_scales[:].indirect(piece))
        for g in range(S // GATHER):
            piece = slot_list[:, g * GATHER // 16 : (g + 1) * GATHER // 16]
            slot_words.append(keep.tile([P, GATHER], U32, name="slot_words%d" % g, align_bytes=64))
            nc.vector.tensor_copy(slot_words[g][:], tok_words[:].bitcast(U32).indirect(piece))

        def quantise(values, width, tag, depth=3):
            codes = work.tile([P, width], U32, name="codes", tag=tag + "_codes", align_bytes=64, bufs=depth)
            scales = work.tile([P, width], U8, name="scales", tag=tag + "_scales", align_bytes=64, bufs=depth)
            nc.vector.quantize_mx(out=codes[:].bitcast(FP8X4), scales=scales[:], in_=values[:])
            return codes, scales

        def first_matrix(name, e, copies):
            rounded = work.tile([P, PACK * H], BF16, name="rounded", tag=name + "_bf16", align_bytes=64)
            turned = rounded[:].rearrange("p (t m j) -> p m j t", t=PACK, j=PACK)
            share = P // len(copies)
            for part, copy in enumerate(copies):
                copy(
                    turned[:, part * share : (part + 1) * share],
                    raw[name, e][part][:].rearrange("p j (m t) -> p m j t", t=PACK),
                )
            return quantise(rounded, H, name)

        def first_product(weights, slot0, tag):
            codes, scales = weights
            bank = psum.tile([P, PACK, P], F32, name="bank", tag=tag)
            g, c0 = divmod(slot0, GATHER)
            for t in range(PACK):
                nc.tensor.matmul_mx(
                    out=bank[:, t, :],
                    lhsT=codes[:, t * P : (t + 1) * P].bitcast(FP8X4),
                    lhsT_scale=scales[:, t * P : (t + 1) * P],
                    rhs=slot_words[g][:, c0 : c0 + P].bitcast(FP8X4),
                    rhs_scale=slot_scales[g][:, c0 : c0 + P],
                    start=True,
                    stop=True,
                )
            return bank

        def first_weights(e):
            q1 = first_matrix("w1", e, [nc.scalar.copy if e == 0 else nc.vector.tensor_copy])
            q3 = first_matrix("w3", e, [nc.scalar.copy, nc.vector.tensor_copy] if e == E - 1 else [nc.scalar.copy])
            return q1, q3

        def hidden(e, q1, q3):
            h = work.tile([P, C * PACK], BF16, name="h", align_bytes=64)
            for half in range(C // P):
                a1 = first_product(q1, e * C + half * P, "a1")
                a3 = first_product(q3, e * C + half * P, "a3")
                act = work.tile([P, P, PACK], F32, name="act")
                nc.scalar.activation(act[:], a1[:].rearrange("p t s -> p s t"), GELU)
                nc.vector.tensor_tensor(
                    h[:, half * P * PACK : (half + 1) * P * PACK].rearrange("p (s t) -> p s t", t=PACK),
                    a3[:].rearrange("p t s -> p s t"),
                    act[:],
                    MULT,
                )
            return quantise(h, C, "h", LAG + 2)

        def second_product(e, hq):
            rounded = work.tile([P, PACK * N], BF16, name="rounded2", align_bytes=64)
            nc.scalar.copy(
                rounded[:].rearrange("p (c i j) -> p c j i", i=4, j=PACK),
                raw["w2", e][:].rearrange("p (j c i) -> p c j i", i=4, j=PACK),
            )
            codes, scales = quantise(rounded, N, "w2")
            bank = psum_y.tile([P, C], F32, name="bank_y")
            nc.tensor.matmul_mx(
                out=bank[:],
                lhsT=codes[:].bitcast(FP8X4),
                lhsT_scale=scales[:],
                rhs=hq[0][:].bitcast(FP8X4),
                rhs_scale=hq[1][:],
                start=True,
                stop=True,
            )
            nc.scalar.copy(y[:, e * C : (e + 1) * C], bank[:])

        hq = {}
        wq = {0: first_weights(0)}
        for e in range(E):
            if e + AHEAD < E:
                load_expert(e + AHEAD)
            if e + 1 < E:
                wq[e + 1] = first_weights(e + 1)
            hq[e] = hidden(e, *wq[e])
            if e >= LAG:
                second_product(e - LAG, hq[e - LAG])
        for e in range(E - LAG, E):
            second_product(e, hq[e])

        lists = []
        for r, pos in enumerate((pos1, pos2, pos3)):
            lists.append(keep.tile([P, T // 16], U16, name="pos%d" % r))
            nc.sync.dma_start(lists[r][:], pos)
        ident = keep.tile([P, P], F32, name="ident")
        make_identity(nc, ident[:])

        t0 = 0
        for n, width in enumerate(CHUNKS):
            gates = ring.tile([P, TOP, width], F32, name="raw", tag="raw")
            nc.sync.dma_start(gates[:], gate[:, :, t0 : t0 + width].rearrange("r p t -> p r t"))
            terms = []
            for r in range(TOP):
                terms.append(work.tile([P, width], F32, name="term", tag="term%d" % r))
                nc.vector.tensor_tensor(
                    terms[r][:], y[:].indirect(lists[r][:, t0 // 16 : (t0 + width) // 16]), gates[:, r, :], MULT
                )
            result = work.tile([P, width], F32, name="result")
            if n + 1 < len(CHUNKS):
                turned = psum.tile([P, width], F32, name="turned", tag="a1")
                for b in range(width // P):
                    for r in range(TOP):
                        nc.tensor.matmul(
                            turned[:, b * P : (b + 1) * P],
                            terms[r][:, b * P : (b + 1) * P],
                            ident[:],
                            start=(r == 0),
                            stop=(r == TOP - 1),
                            is_transpose=True,
                        )
                summed = work.tile([P, width], F32, name="summed")
                nc.scalar.copy(summed[:], turned[:])
                back = psum.tile([P, width], F32, name="back", tag="a3")
                for b in range(width // P):
                    nc.tensor.transpose(back[:, b * P : (b + 1) * P], summed[:, b * P : (b + 1) * P], ident[:])
                nc.scalar.copy(result[:], back[:])
            else:
                pair = work.tile([P, width], F32, name="pair")
                nc.vector.tensor_tensor(pair[:], terms[0][:], terms[1][:], ADD)
                nc.vector.tensor_tensor(result[:], pair[:], terms[2][:], ADD)
            nc.sync.dma_start(out[:, t0 : t0 + width], result[:])
            t0 = t0 + width
